import numpy as np
import ml_dtypes


def mxq(x, axis, fmt="e4m3"):
    dtype, down = {"e4m3": (ml_dtypes.float8_e4m3fn, 7), "e5m2": (ml_dtypes.float8_e5m2, 14)}[fmt]
    v = np.moveaxis(np.asarray(x, np.float32).astype(ml_dtypes.bfloat16).astype(np.float64), axis, -1)
    blocks = v.reshape(v.shape[:-1] + (-1, 32))
    amax = np.abs(blocks).max(-1, keepdims=True)
    byte = np.maximum(np.where(amax > 0, np.frexp(amax)[1] - 1 + 127, 0) - down, 1)
    scale = np.exp2(byte - 127.0)
    codes = (blocks / scale).astype(np.float32).astype(dtype).astype(np.float64)
    return np.moveaxis((codes * scale).reshape(v.shape), -1, axis)


WIDE = False


def mx_kscale(k):
    if not WIDE:
        return np.ones(k)
    levels = np.array([30, -30])
    if k % 512:
        return np.exp2(np.random.permutation(np.resize(levels, k // 32))).repeat(32)
    a = np.empty((k // 512, 16))
    for p in range(k // 512):
        a[p, :8] = np.random.permutation(np.resize(levels, 8))
        for g in range(8):
            far = levels[np.abs(levels - a[p, g]) >= 10]
            a[p, g + 8] = far[np.random.randint(len(far))]
    return np.exp2(a.ravel()).repeat(32)


def f64(x):
    return np.asarray(x).astype(np.float64)


def striped(idx):
    return np.tile(np.asarray(idx).reshape(-1, 16).T, (8, 1)).astype(np.uint16)


def unstriped(offs):
    return offs[:16].T.reshape(-1).astype(np.int64)


E2M1 = np.array([0.0, 0.5, 1.0, 1.5, 2.0, 3.0, 4.0, 6.0, -0.0, -0.5, -1.0, -1.5, -2.0, -3.0, -4.0, -6.0])


def pack_weight(w, fmt):
    k, n = w.shape
    w = f64(np.asarray(w, np.float32).astype(ml_dtypes.bfloat16)).reshape(k // 32, 32, n)
    amax = np.abs(w).max(1)
    if fmt == "e4m3":
        byte = np.frexp(amax)[1] - 1 + 127 - 7
    else:
        mant, ex = np.frexp(amax / 6.0)
        byte = np.where(mant > 0.5, ex, ex - 1) + 127
    byte = np.clip(np.where(amax > 0, byte, 1), 1, 254)
    scaled = (w * np.exp2(127.0 - byte)[:, None, :]).reshape(k, n).astype(np.float32)
    by_word = np.ascontiguousarray(scaled.reshape(k // 512, 128, 4, n).transpose(0, 1, 3, 2))
    if fmt == "e4m3":
        words = by_word.astype(ml_dtypes.float8_e4m3fn).view(np.uint8)
    else:
        c = by_word.astype(ml_dtypes.float4_e2m1fn).view(np.uint8) & 0xF
        words = (c[..., 0::2] | (c[..., 1::2] << 4)).reshape(k // 512, 128, 2 * n)
    return np.ascontiguousarray(words), np.ascontiguousarray(byte.astype(np.uint8).reshape(k // 512, 16, n))


def unpack_weight(words, scales, fmt):
    g, _, n = scales.shape
    words = np.ascontiguousarray(words).reshape(g, 128, n, -1)
    if fmt == "e4m3":
        vals = words.view(ml_dtypes.float8_e4m3fn).astype(np.float64)
    else:
        nib = np.empty((g, 128, n, 4), np.uint8)
        nib[..., 0::2] = words & 0xF
        nib[..., 1::2] = words >> 4
        vals = E2M1[nib]
    vals = vals * np.repeat(np.exp2(scales.astype(np.float64) - 127.0), 8, axis=1)[..., None]
    return vals.transpose(0, 1, 3, 2).reshape(g * 512, n)


def sigmoid(v):
    return 1.0 / (1.0 + np.exp(-v))


K, T, J, R, F, Z, N = 512, 512, 256, 512, 512, 1024, 256


def setup_inputs():
    n = np.random.standard_normal
    idx = np.random.permutation(T)[:J]
    idx2 = np.random.permutation(T)[:J]
    idx3 = np.random.permutation(Z)[:J]
    fk = mx_kscale(K)
    fr = mx_kscale(R)
    ff = mx_kscale(F)
    wp = pack_weight(n((K, R)) * 1 / np.sqrt(K) * fk[:, None] * fr, "e2m1")
    w2p = pack_weight(n((F, R)) * 1 / np.sqrt(F) * ff[:, None] * fr, "e2m1")
    wbp = pack_weight(n((R, N)) * 1 / np.sqrt(R) / fr[:, None], "e2m1")
    return {
        "xf": (n((K, T))).astype(np.float32),
        "fk": (np.random.uniform(0.5, 2.0, (K, 1)) / fk[:, None]).astype(np.float32),
        "w_words": wp[0],
        "w_scales": wp[1],
        "xo": (n((F, Z))).astype(np.float32),
        "fl": (np.random.uniform(0.5, 2.0, (F, 1)) / ff[:, None]).astype(np.float32),
        "so": (n((F, J))).astype(np.float32),
        "w2_words": w2p[0],
        "w2_scales": w2p[1],
        "wb_words": wbp[0],
        "wb_scales": wbp[1],
        "rs": (1.0 * n((J, N))).astype(np.float32),
        "offs": striped(idx),
        "offs2": striped(idx2),
        "offs3": striped(idx3),
    }


def reference(xf, fk, w_words, w_scales, xo, fl, so, w2_words, w2_scales, wb_words, wb_scales, rs, offs, offs2, offs3):
    idx = unstriped(offs)
    idx2 = unstriped(offs2)
    idx3 = unstriped(offs3)
    wu = unpack_weight(w_words, w_scales, "e2m1")
    w2u = unpack_weight(w2_words, w2_scales, "e2m1")
    wbu = unpack_weight(wb_words, wb_scales, "e2m1")
    u = np.maximum(f64(xf)[:, idx], f64(xf)[:, idx2]) * f64(fk)
    u2 = f64(xo)[:, idx3] * sigmoid(f64(so)) * f64(fl)
    uq = mxq(u, 0, "e4m3")
    a = wu.T @ uq
    u2q = mxq(u2, 0, "e5m2")
    q = w2u.T @ u2q
    y1 = np.pad(q, ((0, 0), (1, 0)))[:, :J]
    hid = np.maximum(a, q - 0.6 * y1)
    hidq = mxq(hid, 0, "e5m2")
    p = hidq.T @ wbu
    mn = np.mean(np.abs(p), axis=1, keepdims=True)
    y = np.maximum(p - mn, 0.0) - 0.3 * f64(rs)
    return y

@@ -1,0 +1,212 @@
+from contextlib import ExitStack
+
+import concourse.mybir as mybir
+
+K, T, J, R, F, Z, N = 512, 512, 256, 512, 512, 1024, 256
+FLOPS = 2 * (K * R * J + F * R * J + R * J * N)
+
+F32 = mybir.dt.float32
+BF16 = mybir.dt.bfloat16
+I32 = mybir.dt.int32
+U32 = mybir.dt.uint32
+U16 = mybir.dt.uint16
+U8 = mybir.dt.uint8
+E4M3 = mybir.dt.float8_e4m3fn_x4
+E5M2 = mybir.dt.float8_e5m2_x4
+E2M1 = mybir.dt.float4_e2m1fn_x4
+ALU = mybir.AluOpType
+ACT = mybir.ActivationFunctionType
+
+P = 128
+PACK = 4
+HALF = 128
+
+
+def tile_list_two_largerpicks_gated_stepgap_rowabove_kernel(
+    tc, xf, fk, w_words, w_scales, xo, fl, so, w2_words, w2_scales, wb_words, wb_scales, rs, offs, offs2, offs3, out
+):
+    nc = tc.nc
+    with ExitStack() as ctx:
+        sb = ctx.enter_context(tc.tile_pool(name="sb", bufs=1))
+        ps = ctx.enter_context(tc.psum_pool(name="ps", bufs=1))
+
+        def new(name, shape, dtype):
+            return sb.tile(shape, dtype, name=name, align_bytes=64)
+
+        list1 = new("list1", [P, J // 16], U16)
+        list2 = new("list2", [P, J // 16], U16)
+        list3 = new("list3", [P, J // 16], U16)
+        so_sb = new("so_sb", [P, PACK * J], F32)
+        xf_sb = [new("xf_sb%d" % t, [P, T], F32) for t in range(PACK)]
+        xo_sb = [new("xo_sb%d" % t, [P, Z], F32) for t in range(PACK)]
+        fk_sb = new("fk_sb", [P, PACK], F32)
+        fl_sb = new("fl_sb", [P, PACK], F32)
+        w_raw = new("w_raw", [P, 2 * R], U8)
+        w2_raw = new("w2_raw", [P, 2 * R], U8)
+        wb_sb = new("wb_sb", [P, 2 * N], U8)
+        ws_raw = new("ws_raw", [P, R], U8)
+        w2s_raw = new("w2s_raw", [P, R], U8)
+        wbs_sb = new("wbs_sb", [P, N], U8)
+        rs_sb = new("rs_sb", [P, 2, N], F32)
+        q_sb = new("q_sb", [P, PACK * (J + 1)], F32)
+
+        def load_scales(engine, plane, scales):
+            for quad in range(4):
+                engine.dma_start(
+                    out=plane[32 * quad : 32 * quad + 4, :].bitcast(I32),
+                    in_=scales[0, 4 * quad : 4 * quad + 4, :].bitcast(I32),
+                )
+
+        for plane in (w2s_raw, ws_raw, wbs_sb):
+            nc.gpsimd.memset(plane[:].bitcast(U32), 0)
+        nc.gpsimd.memset(q_sb[:, 0:PACK], 0.0)
+        load_scales(nc.gpsimd, w2s_raw, w2_scales)
+        load_scales(nc.gpsimd, ws_raw, w_scales)
+
+        xf_rows = xf.rearrange("(p t) c -> p t c", t=PACK)
+        xo_rows = xo.rearrange("(p t) c -> p t c", t=PACK)
+        nc.sync.dma_start(out=so_sb[:], in_=so.rearrange("(p t) j -> p (t j)", t=PACK))
+        nc.sync.dma_start(out=list1[:], in_=offs)
+        nc.sync.dma_start(out=list2[:], in_=offs2)
+        for t in range(PACK):
+            nc.sync.dma_start(out=xf_sb[t][:], in_=xf_rows[:, t, :])
+        nc.sync.dma_start(out=fk_sb[:], in_=fk.rearrange("(p t) o -> p (t o)", t=PACK))
+        nc.sync.dma_start(out=xo_sb[0][:], in_=xo_rows[:, 0, :])
+        nc.sync.dma_start(out=list3[:], in_=offs3)
+        nc.sync.dma_start(out=fl_sb[:], in_=fl.rearrange("(p t) o -> p (t o)", t=PACK))
+        nc.sync.dma_start(out=w2_raw[:].bitcast(I32), in_=w2_words[0].bitcast(I32))
+        nc.sync.dma_start(out=w_raw[:].bitcast(I32), in_=w_words[0].bitcast(I32))
+        for t in range(1, PACK):
+            nc.sync.dma_start(out=xo_sb[t][:], in_=xo_rows[:, t, :])
+        nc.sync.dma_start(out=wb_sb[:].bitcast(I32), in_=wb_words[0].bitcast(I32))
+        load_scales(nc.sync, wbs_sb, wb_scales)
+        nc.sync.dma_start(out=rs_sb[:], in_=rs.rearrange("(h p) n -> p h n", p=P))
+
+        gate = new("gate", [P, PACK, J], F32)
+        nc.scalar.activation(out=gate[:].rearrange("p t j -> p (t j)"), in_=so_sb[:], func=ACT.Sigmoid)
+
+        pick1 = new("pick1", [P, PACK, J], F32)
+        pick2 = new("pick2", [P, PACK, J], F32)
+        larger = new("larger", [P, PACK, J], F32)
+        for t in range(PACK):
+            nc.scalar.activation(out=pick1[:, t, :], in_=xf_sb[t][:].indirect(list1[:]), func=ACT.Copy)
+            nc.vector.tensor_copy(out=pick2[:, t, :], in_=xf_sb[t][:].indirect(list2[:]))
+        for t in range(0, PACK, 2):
+            nc.vector.tensor_tensor(
+                out=larger[:, t : t + 2, :], in0=pick1[:, t : t + 2, :], in1=pick2[:, t : t + 2, :], op=ALU.max
+            )
+        u_bf = new("u_bf", [P, J * PACK], BF16)
+        nc.vector.tensor_tensor(
+            out=u_bf[:].rearrange("p (c i t) -> p c t i", i=4, t=PACK),
+            in0=larger[:].rearrange("p t (c i) -> p c t i", i=4),
+            in1=fk_sb[:].unsqueeze(1).unsqueeze(3).to_broadcast([P, J // 4, PACK, 4]),
+            op=ALU.mult,
+        )
+        u_codes = new("u_codes", [P, J], U32)
+        u_scales = new("u_scales", [P, J], U8)
+        nc.vector.quantize_mx(out=u_codes[:].bitcast(E4M3), scales=u_scales[:], in_=u_bf[:])
+
+        def deal(name, raw_words, raw_scales):
+            words = new(name + "_dealt", [P, 2 * R], U8)
+            scales = new(name + "s_dealt", [P, R], U8)
+            nc.scalar.copy(
+                out=words[:].bitcast(U16).rearrange("p (t m) -> p t m", t=PACK),
+                in_=raw_words[:].bitcast(U16).rearrange("p (m t) -> p t m", t=PACK),
+            )
+            nc.vector.tensor_copy(
+                out=scales[:].rearrange("p (t m) -> p t m", t=PACK),
+                in_=raw_scales[:].rearrange("p (m t) -> p t m", t=PACK),
+            )
+            return words, scales
+
+        w2_dealt, w2s_dealt = deal("w2", w2_raw, w2s_raw)
+        w_dealt, ws_dealt = deal("w", w_raw, ws_raw)
+
+        def product(bank, words, scales, codes, code_scales):
+            for t in range(PACK):
+                nc.tensor.matmul_mx(
+                    out=bank[:, t, :],
+                    lhsT=words[:, 2 * P * t : 2 * P * (t + 1)].bitcast(E2M1),
+                    lhsT_scale=scales[:, P * t : P * (t + 1)],
+                    rhs=codes,
+                    rhs_scale=code_scales,
+                    start=True,
+                    stop=True,
+                )
+
+        a_ps = [ps.tile([P, PACK, HALF], F32, name="a_ps%d" % h) for h in range(2)]
+        for h in range(2):
+            cols = slice(HALF * h, HALF * (h + 1))
+            product(a_ps[h], w_dealt, ws_dealt, u_codes[:, cols].bitcast(E4M3), u_scales[:, cols])
+
+        entry = new("entry", [P, PACK, J], F32)
+        gated = new("gated", [P, PACK, J], F32)
+
+        def gate_entries(t, cols):
+            nc.vector.scalar_tensor_tensor(
+                out=gated[:, t, cols], in0=entry[:, t, cols], scalar=fl_sb[:, t : t + 1], in1=gate[:, t, cols],
+                op0=ALU.mult, op1=ALU.mult,
+            )
+
+        last = PACK - 1
+        for t in range(last):
+            nc.scalar.activation(out=entry[:, t, :], in_=xo_sb[t][:].indirect(list3[:]), func=ACT.Copy)
+            gate_entries(t, slice(0, J))
+        nc.scalar.activation(out=entry[:, last, 0:HALF], in_=xo_sb[last][:].indirect(list3[:, 0:8]), func=ACT.Copy)
+        nc.vector.tensor_copy(out=entry[:, last, HALF:J], in_=xo_sb[last][:].indirect(list3[:, 8:16]))
+        halves = [slice(HALF * h, HALF * (h + 1)) for h in range(2)]
+        for cols in halves:
+            gate_entries(last, cols)
+        u2_bf = [new("u2_bf%d" % h, [P, HALF * PACK], BF16) for h in range(2)]
+        for h in range(2):
+            nc.vector.tensor_copy(
+                out=u2_bf[h][:].rearrange("p (c i t) -> p c t i", i=4, t=PACK),
+                in_=gated[:, :, halves[h]].rearrange("p t (c i) -> p c t i", i=4),
+            )
+        q_ps = [ps.tile([P, PACK, HALF], F32, name="q_ps%d" % h) for h in range(2)]
+        for h in range(2):
+            codes = new("u2_codes%d" % h, [P, HALF], U32)
+            scales = new("u2_scales%d" % h, [P, HALF], U8)
+            nc.vector.quantize_mx(out=codes[:].bitcast(E5M2), scales=scales[:], in_=u2_bf[h][:])
+            product(q_ps[h], w2_dealt, w2s_dealt, codes[:].bitcast(E5M2), scales[:])
+
+        W = HALF * PACK
+        step = [new("step%d" % h, [P, W], F32) for h in range(2)]
+        hid_bf = [new("hid_bf%d" % h, [P, W], BF16) for h in range(2)]
+        for h in range(2):
+            nc.scalar.copy(
+                out=q_sb[:, PACK + W * h : PACK + W * (h + 1)].rearrange("p (j t) -> p j t", t=PACK),
+                in_=q_ps[h][:].rearrange("p t j -> p j t"),
+            )
+        for h in range(2):
+            nc.vector.scalar_tensor_tensor(
+                out=step[h][:], in0=q_sb[:, W * h : W * (h + 1)], scalar=-0.6,
+                in1=q_sb[:, PACK + W * h : PACK + W * (h + 1)], op0=ALU.mult, op1=ALU.add,
+            )
+        for h in range(2):
+            nc.vector.tensor_tensor(
+                out=hid_bf[h][:].rearrange("p (j t) -> p j t", t=PACK),
+                in0=a_ps[h][:].rearrange("p t j -> p j t"),
+                in1=step[h][:].rearrange("p (j t) -> p j t", t=PACK),
+                op=ALU.max,
+            )
+        p_ps = [ps.tile([P, N], F32, name="p_ps%d" % h) for h in range(2)]
+        for h in range(2):
+            codes = new("hid_codes%d" % h, [P, HALF], U32)
+            scales = new("hid_scales%d" % h, [P, HALF], U8)
+            nc.vector.quantize_mx(out=codes[:].bitcast(E5M2), scales=scales[:], in_=hid_bf[h][:])
+            nc.tensor.matmul_mx(
+                out=p_ps[h][:], lhsT=codes[:].bitcast(E5M2), lhsT_scale=scales[:],
+                rhs=wb_sb[:].bitcast(E2M1), rhs_scale=wbs_sb[:], start=True, stop=True,
+            )
+        for h in range(2):
+            magnitude = new("magnitude%d" % h, [P, N], F32)
+            mean = new("mean%d" % h, [P, 1], F32)
+            nc.scalar.activation(out=magnitude[:], in_=p_ps[h][:], func=ACT.Abs, scale=1.0 / N, accum_out=mean[:])
+            taken = new("taken%d" % h, [P, N], F32)
+            nc.scalar.activation(out=taken[:], in_=rs_sb[:, h, :], func=ACT.Identity, scale=0.3, bias=mean[:])
+            result = new("result%d" % h, [P, N], F32)
+            nc.vector.scalar_tensor_tensor(
+                out=result[:], in0=p_ps[h][:], scalar=mean[:], in1=taken[:], op0=ALU.max, op1=ALU.subtract
+            )
+            nc.sync.dma_start(out=out[halves[h], :], in_=result[:])

@@ -30,13 +30,14 @@ def tile_list_two_largerpicks_gated_stepgap_rowabove_kernel(
         sb = ctx.enter_context(tc.tile_pool(name="sb", bufs=1))
         ps = ctx.enter_context(tc.psum_pool(name="ps", bufs=1))
 
-        def new(name, shape, dtype):
-            return sb.tile(shape, dtype, name=name, align_bytes=64)
+        def new(name, shape, dtype, tag=None):
+            return sb.tile(shape, dtype, name=name, tag=tag or name, align_bytes=64)
 
         list1 = new("list1", [P, J // 16], U16)
         list2 = new("list2", [P, J // 16], U16)
         list3 = new("list3", [P, J // 16], U16)
-        so_sb = new("so_sb", [P, PACK * J], F32)
+        so_first = new("so_first", [P, J], F32)
+        so_rest = new("so_rest", [P, (PACK - 1) * J], F32)
         xf_sb = [new("xf_sb%d" % t, [P, T], F32) for t in range(PACK)]
         xo_sb = [new("xo_sb%d" % t, [P, Z], F32) for t in range(PACK)]
         fk_sb = new("fk_sb", [P, PACK], F32)
@@ -50,77 +51,96 @@ def tile_list_two_largerpicks_gated_stepgap_rowabove_kernel(
         rs_sb = new("rs_sb", [P, 2, N], F32)
         q_sb = new("q_sb", [P, PACK * (J + 1)], F32)
 
-        def load_scales(engine, plane, scales):
-            for quad in range(4):
-                engine.dma_start(
-                    out=plane[32 * quad : 32 * quad + 4, :].bitcast(I32),
-                    in_=scales[0, 4 * quad : 4 * quad + 4, :].bitcast(I32),
-                )
+        def load_scales(plane, scales, quad):
+            nc.sync.dma_start(
+                out=plane[32 * quad : 32 * quad + 4, :].bitcast(I32),
+                in_=scales[0, 4 * quad : 4 * quad + 4, :].bitcast(I32),
+            )
 
         for plane in (w2s_raw, ws_raw, wbs_sb):
             nc.gpsimd.memset(plane[:].bitcast(U32), 0)
         nc.gpsimd.memset(q_sb[:, 0:PACK], 0.0)
-        load_scales(nc.gpsimd, w2s_raw, w2_scales)
-        load_scales(nc.gpsimd, ws_raw, w_scales)
 
         xf_rows = xf.rearrange("(p t) c -> p t c", t=PACK)
         xo_rows = xo.rearrange("(p t) c -> p t c", t=PACK)
-        nc.sync.dma_start(out=so_sb[:], in_=so.rearrange("(p t) j -> p (t j)", t=PACK))
+        so_rows = so.rearrange("(p t) j -> p (t j)", t=PACK)
+        nc.sync.dma_start(out=so_first[:], in_=so_rows[:, 0:J])
         nc.sync.dma_start(out=list1[:], in_=offs)
         nc.sync.dma_start(out=list2[:], in_=offs2)
-        for t in range(PACK):
-            nc.sync.dma_start(out=xf_sb[t][:], in_=xf_rows[:, t, :])
+        nc.sync.dma_start(out=xf_sb[0][:], in_=xf_rows[:, 0, :])
+        nc.sync.dma_start(out=w2_raw[:].bitcast(I32), in_=w2_words[0].bitcast(I32))
+        nc.sync.dma_start(out=xf_sb[1][:], in_=xf_rows[:, 1, :])
+        load_scales(w2s_raw, w2_scales, 0)
+        load_scales(w2s_raw, w2_scales, 1)
+        nc.sync.dma_start(out=xf_sb[2][:], in_=xf_rows[:, 2, :])
+        load_scales(w2s_raw, w2_scales, 2)
+        load_scales(w2s_raw, w2_scales, 3)
+        nc.sync.dma_start(out=xf_sb[3][:], in_=xf_rows[:, 3, :])
         nc.sync.dma_start(out=fk_sb[:], in_=fk.rearrange("(p t) o -> p (t o)", t=PACK))
-        nc.sync.dma_start(out=xo_sb[0][:], in_=xo_rows[:, 0, :])
+        nc.sync.dma_start(out=so_rest[:], in_=so_rows[:, J : PACK * J])
         nc.sync.dma_start(out=list3[:], in_=offs3)
         nc.sync.dma_start(out=fl_sb[:], in_=fl.rearrange("(p t) o -> p (t o)", t=PACK))
-        nc.sync.dma_start(out=w2_raw[:].bitcast(I32), in_=w2_words[0].bitcast(I32))
-        nc.sync.dma_start(out=w_raw[:].bitcast(I32), in_=w_words[0].bitcast(I32))
-        for t in range(1, PACK):
+        for t in range(PACK):
             nc.sync.dma_start(out=xo_sb[t][:], in_=xo_rows[:, t, :])
+        nc.sync.dma_start(out=w_raw[:].bitcast(I32), in_=w_words[0].bitcast(I32))
+        for quad in range(4):
+            load_scales(ws_raw, w_scales, quad)
         nc.sync.dma_start(out=wb_sb[:].bitcast(I32), in_=wb_words[0].bitcast(I32))
-        load_scales(nc.sync, wbs_sb, wb_scales)
+        for quad in range(4):
+            load_scales(wbs_sb, wb_scales, quad)
         nc.sync.dma_start(out=rs_sb[:], in_=rs.rearrange("(h p) n -> p h n", p=P))
 
+        def deal_words(name, raw_words, tag=None):
+            words = new(name, [P, 2 * R], U8, tag)
+            nc.scalar.copy(
+                out=words[:].bitcast(U16).rearrange("p (t m) -> p t m", t=PACK),
+                in_=raw_words[:].bitcast(U16).rearrange("p (m t) -> p t m", t=PACK),
+            )
+            return words
+
+        def deal_scales(name, raw_scales, tag):
+            scales = new(name, [P, R], U8, tag)
+            nc.vector.tensor_copy(
+                out=scales[:].rearrange("p (t m) -> p t m", t=PACK),
+                in_=raw_scales[:].rearrange("p (m t) -> p t m", t=PACK),
+            )
+            return scales
+
         gate = new("gate", [P, PACK, J], F32)
-        nc.scalar.activation(out=gate[:].rearrange("p t j -> p (t j)"), in_=so_sb[:], func=ACT.Sigmoid)
+        nc.scalar.activation(out=gate[:, 0, :], in_=so_first[:], func=ACT.Sigmoid)
 
         pick1 = new("pick1", [P, PACK, J], F32)
         pick2 = new("pick2", [P, PACK, J], F32)
         larger = new("larger", [P, PACK, J], F32)
         for t in range(PACK):
             nc.scalar.activation(out=pick1[:, t, :], in_=xf_sb[t][:].indirect(list1[:]), func=ACT.Copy)
-            nc.vector.tensor_copy(out=pick2[:, t, :], in_=xf_sb[t][:].indirect(list2[:]))
+            if t < PACK - 1:
+                nc.vector.tensor_copy(out=pick2[:, t, :], in_=xf_sb[t][:].indirect(list2[:]))
+            else:
+                nc.scalar.activation(out=pick2[:, t, :], in_=xf_sb[t][:].indirect(list2[:]), func=ACT.Copy)
         for t in range(0, PACK, 2):
             nc.vector.tensor_tensor(
                 out=larger[:, t : t + 2, :], in0=pick1[:, t : t + 2, :], in1=pick2[:, t : t + 2, :], op=ALU.max
             )
-        u_bf = new("u_bf", [P, J * PACK], BF16)
-        nc.vector.tensor_tensor(
-            out=u_bf[:].rearrange("p (c i t) -> p c t i", i=4, t=PACK),
-            in0=larger[:].rearrange("p t (c i) -> p c t i", i=4),
-            in1=fk_sb[:].unsqueeze(1).unsqueeze(3).to_broadcast([P, J // 4, PACK, 4]),
-            op=ALU.mult,
-        )
+        halves = [slice(HALF * h, HALF * (h + 1)) for h in range(2)]
+        u_bf = [new("u_bf%d" % h, [P, HALF * PACK], BF16) for h in range(2)]
         u_codes = new("u_codes", [P, J], U32)
         u_scales = new("u_scales", [P, J], U8)
-        nc.vector.quantize_mx(out=u_codes[:].bitcast(E4M3), scales=u_scales[:], in_=u_bf[:])
-
-        def deal(name, raw_words, raw_scales):
-            words = new(name + "_dealt", [P, 2 * R], U8)
-            scales = new(name + "s_dealt", [P, R], U8)
-            nc.scalar.copy(
-                out=words[:].bitcast(U16).rearrange("p (t m) -> p t m", t=PACK),
-                in_=raw_words[:].bitcast(U16).rearrange("p (m t) -> p t m", t=PACK),
+        for h in range(2):
+            nc.vector.tensor_tensor(
+                out=u_bf[h][:].rearrange("p (c i t) -> p c t i", i=4, t=PACK),
+                in0=larger[:, :, halves[h]].rearrange("p t (c i) -> p c t i", i=4),
+                in1=fk_sb[:].unsqueeze(1).unsqueeze(3).to_broadcast([P, HALF // 4, PACK, 4]),
+                op=ALU.mult,
             )
-            nc.vector.tensor_copy(
-                out=scales[:].rearrange("p (t m) -> p t m", t=PACK),
-                in_=raw_scales[:].rearrange("p (m t) -> p t m", t=PACK),
+        for h in range(2):
+            nc.vector.quantize_mx(
+                out=u_codes[:, halves[h]].bitcast(E4M3), scales=u_scales[:, halves[h]], in_=u_bf[h][:]
             )
-            return words, scales
 
-        w2_dealt, w2s_dealt = deal("w2", w2_raw, w2s_raw)
-        w_dealt, ws_dealt = deal("w", w_raw, ws_raw)
+        w2s_dealt = deal_scales("w2s_dealt", w2s_raw, "pick2")
+        w2_dealt = deal_words("w2_dealt", w2_raw)
+        nc.scalar.activation(out=gate[:, 1:PACK, :].rearrange("p t j -> p (t j)"), in_=so_rest[:], func=ACT.Sigmoid)
 
         def product(bank, words, scales, codes, code_scales):
             for t in range(PACK):
@@ -134,29 +154,24 @@ def tile_list_two_largerpicks_gated_stepgap_rowabove_kernel(
                     stop=True,
                 )
 
-        a_ps = [ps.tile([P, PACK, HALF], F32, name="a_ps%d" % h) for h in range(2)]
-        for h in range(2):
-            cols = slice(HALF * h, HALF * (h + 1))
-            product(a_ps[h], w_dealt, ws_dealt, u_codes[:, cols].bitcast(E4M3), u_scales[:, cols])
+        last = PACK - 1
+        entry = new("entry", [P, last, J], F32)
+        entry_end = [new("entry_end0", [P, HALF], F32), new("entry_end1", [P, HALF], F32, "u_bf1")]
+        gated = new("gated", [P, PACK, J], F32, "u_bf0")
 
-        entry = new("entry", [P, PACK, J], F32)
-        gated = new("gated", [P, PACK, J], F32)
-
-        def gate_entries(t, cols):
+        def gate_entries(picked, t, cols):
             nc.vector.scalar_tensor_tensor(
-                out=gated[:, t, cols], in0=entry[:, t, cols], scalar=fl_sb[:, t : t + 1], in1=gate[:, t, cols],
+                out=gated[:, t, cols], in0=picked, scalar=fl_sb[:, t : t + 1], in1=gate[:, t, cols],
                 op0=ALU.mult, op1=ALU.mult,
             )
 
-        last = PACK - 1
         for t in range(last):
             nc.scalar.activation(out=entry[:, t, :], in_=xo_sb[t][:].indirect(list3[:]), func=ACT.Copy)
-            gate_entries(t, slice(0, J))
-        nc.scalar.activation(out=entry[:, last, 0:HALF], in_=xo_sb[last][:].indirect(list3[:, 0:8]), func=ACT.Copy)
-        nc.vector.tensor_copy(out=entry[:, last, HALF:J], in_=xo_sb[last][:].indirect(list3[:, 8:16]))
-        halves = [slice(HALF * h, HALF * (h + 1)) for h in range(2)]
-        for cols in halves:
-            gate_entries(last, cols)
+            gate_entries(entry[:, t, :], t, slice(0, J))
+        nc.scalar.activation(out=entry_end[0][:], in_=xo_sb[last][:].indirect(list3[:, 0:8]), func=ACT.Copy)
+        nc.vector.tensor_copy(out=entry_end[1][:], in_=xo_sb[last][:].indirect(list3[:, 8:16]))
+        for h in range(2):
+            gate_entries(entry_end[h][:], last, halves[h])
         u2_bf = [new("u2_bf%d" % h, [P, HALF * PACK], BF16) for h in range(2)]
         for h in range(2):
             nc.vector.tensor_copy(
@@ -169,6 +184,13 @@ def tile_list_two_largerpicks_gated_stepgap_rowabove_kernel(
             scales = new("u2_scales%d" % h, [P, HALF], U8)
             nc.vector.quantize_mx(out=codes[:].bitcast(E5M2), scales=scales[:], in_=u2_bf[h][:])
             product(q_ps[h], w2_dealt, w2s_dealt, codes[:].bitcast(E5M2), scales[:])
+
+        w_dealt = deal_words("w_dealt", w_raw, "entry_end0")
+        ws_dealt = deal_scales("ws_dealt", ws_raw, "u2_bf1")
+        a_ps = [ps.tile([P, PACK, HALF], F32, name="a_ps%d" % h) for h in range(2)]
+        for h in range(2):
+            cols = slice(HALF * h, HALF * (h + 1))
+            product(a_ps[h], w_dealt, ws_dealt, u_codes[:, cols].bitcast(E4M3), u_scales[:, cols])
 
         W = HALF * PACK
         step = [new("step%d" % h, [P, W], F32) for h in range(2)]
@@ -199,14 +221,22 @@ def tile_list_two_largerpicks_gated_stepgap_rowabove_kernel(
                 out=p_ps[h][:], lhsT=codes[:].bitcast(E5M2), lhsT_scale=scales[:],
                 rhs=wb_sb[:].bitcast(E2M1), rhs_scale=wbs_sb[:], start=True, stop=True,
             )
+        mean = [new("mean%d" % h, [P, 1], F32) for h in range(2)]
+        result = [new("result%d" % h, [P, N], F32) for h in range(2)]
         for h in range(2):
             magnitude = new("magnitude%d" % h, [P, N], F32)
-            mean = new("mean%d" % h, [P, 1], F32)
-            nc.scalar.activation(out=magnitude[:], in_=p_ps[h][:], func=ACT.Abs, scale=1.0 / N, accum_out=mean[:])
-            taken = new("taken%d" % h, [P, N], F32)
-            nc.scalar.activation(out=taken[:], in_=rs_sb[:, h, :], func=ACT.Identity, scale=0.3, bias=mean[:])
-            result = new("result%d" % h, [P, N], F32)
-            nc.vector.scalar_tensor_tensor(
-                out=result[:], in0=p_ps[h][:], scalar=mean[:], in1=taken[:], op0=ALU.max, op1=ALU.subtract
-            )
-            nc.sync.dma_start(out=out[halves[h], :], in_=result[:])
+            nc.scalar.activation(out=magnitude[:], in_=p_ps[h][:], func=ACT.Abs, scale=1.0 / N, accum_out=mean[h][:])
+        above = new("above", [P, N], F32)
+        nc.vector.tensor_scalar(
+            out=above[:], in0=p_ps[0][:], scalar1=mean[0][:], scalar2=0.0, op0=ALU.subtract, op1=ALU.max
+        )
+        nc.vector.scalar_tensor_tensor(
+            out=result[0][:], in0=rs_sb[:, 0, :], scalar=-0.3, in1=above[:], op0=ALU.mult, op1=ALU.add
+        )
+        nc.sync.dma_start(out=out[halves[0], :], in_=result[0][:])
+        taken = new("taken", [P, N], F32)
+        nc.scalar.activation(out=taken[:], in_=rs_sb[:, 1, :], func=ACT.Identity, scale=0.3, bias=mean[1][:])
+        nc.vector.scalar_tensor_tensor(
+            out=result[1][:], in0=p_ps[1][:], scalar=mean[1][:], in1=taken[:], op0=ALU.max, op1=ALU.subtract
+        )
+        nc.sync.dma_start(out=out[halves[1], :], in_=result[1][:])

@@ -38,8 +38,11 @@ def tile_list_two_largerpicks_gated_stepgap_rowabove_kernel(
         list3 = new("list3", [P, J // 16], U16)
         so_first = new("so_first", [P, J], F32)
         so_rest = new("so_rest", [P, (PACK - 1) * J], F32)
-        xf_sb = [new("xf_sb%d" % t, [P, T], F32) for t in range(PACK)]
-        xo_sb = [new("xo_sb%d" % t, [P, Z], F32) for t in range(PACK)]
+        xf_pair = [new("xf_pair%d" % g, [P, 2 * T], F32) for g in range(2)]
+        xf_sb = [xf_pair[t // 2][:, T * (t % 2) : T * (t % 2 + 1)] for t in range(PACK)]
+        xo_pair = new("xo_pair", [P, 2 * Z], F32)
+        xo_single = [new("xo_single%d" % t, [P, Z], F32) for t in range(2)]
+        xo_sb = [xo_pair[:, 0:Z], xo_pair[:, Z : 2 * Z], xo_single[0][:], xo_single[1][:]]
         fk_sb = new("fk_sb", [P, PACK], F32)
         fl_sb = new("fl_sb", [P, PACK], F32)
         w_raw = new("w_raw", [P, 2 * R], U8)
@@ -51,43 +54,40 @@ def tile_list_two_largerpicks_gated_stepgap_rowabove_kernel(
         rs_sb = new("rs_sb", [P, 2, N], F32)
         q_sb = new("q_sb", [P, PACK * (J + 1)], F32)
 
-        def load_scales(plane, scales, quad):
-            nc.sync.dma_start(
+        def load_scales(queue, plane, scales, quad):
+            queue.dma_start(
                 out=plane[32 * quad : 32 * quad + 4, :].bitcast(I32),
                 in_=scales[0, 4 * quad : 4 * quad + 4, :].bitcast(I32),
             )
 
         for plane in (w2s_raw, ws_raw, wbs_sb):
-            nc.gpsimd.memset(plane[:].bitcast(U32), 0)
-        nc.gpsimd.memset(q_sb[:, 0:PACK], 0.0)
+            nc.vector.memset(plane[:].bitcast(U32), 0)
+        nc.vector.memset(q_sb[:, 0:PACK], 0.0)
 
-        xf_rows = xf.rearrange("(p t) c -> p t c", t=PACK)
-        xo_rows = xo.rearrange("(p t) c -> p t c", t=PACK)
+        xf_rows = xf.rearrange("(p t) c -> p (t c)", t=PACK)
+        xo_rows = xo.rearrange("(p t) c -> p (t c)", t=PACK)
         so_rows = so.rearrange("(p t) j -> p (t j)", t=PACK)
+        for quad in range(4):
+            load_scales(nc.gpsimd, w2s_raw, w2_scales, quad)
+        for quad in range(4):
+            load_scales(nc.gpsimd, ws_raw, w_scales, quad)
         nc.sync.dma_start(out=so_first[:], in_=so_rows[:, 0:J])
         nc.sync.dma_start(out=list1[:], in_=offs)
         nc.sync.dma_start(out=list2[:], in_=offs2)
-        nc.sync.dma_start(out=xf_sb[0][:], in_=xf_rows[:, 0, :])
-        nc.sync.dma_start(out=w2_raw[:].bitcast(I32), in_=w2_words[0].bitcast(I32))
-        nc.sync.dma_start(out=xf_sb[1][:], in_=xf_rows[:, 1, :])
-        load_scales(w2s_raw, w2_scales, 0)
-        load_scales(w2s_raw, w2_scales, 1)
-        nc.sync.dma_start(out=xf_sb[2][:], in_=xf_rows[:, 2, :])
-        load_scales(w2s_raw, w2_scales, 2)
-        load_scales(w2s_raw, w2_scales, 3)
-        nc.sync.dma_start(out=xf_sb[3][:], in_=xf_rows[:, 3, :])
+        for g in range(2):
+            nc.sync.dma_start(out=xf_pair[g][:], in_=xf_rows[:, 2 * T * g : 2 * T * (g + 1)])
         nc.sync.dma_start(out=fk_sb[:], in_=fk.rearrange("(p t) o -> p (t o)", t=PACK))
         nc.sync.dma_start(out=so_rest[:], in_=so_rows[:, J : PACK * J])
         nc.sync.dma_start(out=list3[:], in_=offs3)
+        nc.sync.dma_start(out=xo_pair[:], in_=xo_rows[:, 0 : 2 * Z])
         nc.sync.dma_start(out=fl_sb[:], in_=fl.rearrange("(p t) o -> p (t o)", t=PACK))
-        for t in range(PACK):
-            nc.sync.dma_start(out=xo_sb[t][:], in_=xo_rows[:, t, :])
+        for t in range(2):
+            nc.sync.dma_start(out=xo_single[t][:], in_=xo_rows[:, Z * (2 + t) : Z * (3 + t)])
+        nc.sync.dma_start(out=w2_raw[:].bitcast(I32), in_=w2_words[0].bitcast(I32))
         nc.sync.dma_start(out=w_raw[:].bitcast(I32), in_=w_words[0].bitcast(I32))
-        for quad in range(4):
-            load_scales(ws_raw, w_scales, quad)
         nc.sync.dma_start(out=wb_sb[:].bitcast(I32), in_=wb_words[0].bitcast(I32))
         for quad in range(4):
-            load_scales(wbs_sb, wb_scales, quad)
+            load_scales(nc.sync, wbs_sb, wb_scales, quad)
         nc.sync.dma_start(out=rs_sb[:], in_=rs.rearrange("(h p) n -> p h n", p=P))
 
         def deal_words(name, raw_words, tag=None):
@@ -113,11 +113,11 @@ def tile_list_two_largerpicks_gated_stepgap_rowabove_kernel(
         pick2 = new("pick2", [P, PACK, J], F32)
         larger = new("larger", [P, PACK, J], F32)
         for t in range(PACK):
-            nc.scalar.activation(out=pick1[:, t, :], in_=xf_sb[t][:].indirect(list1[:]), func=ACT.Copy)
+            nc.scalar.activation(out=pick1[:, t, :], in_=xf_sb[t].indirect(list1[:]), func=ACT.Copy)
             if t < PACK - 1:
-                nc.vector.tensor_copy(out=pick2[:, t, :], in_=xf_sb[t][:].indirect(list2[:]))
+                nc.vector.tensor_copy(out=pick2[:, t, :], in_=xf_sb[t].indirect(list2[:]))
             else:
-                nc.scalar.activation(out=pick2[:, t, :], in_=xf_sb[t][:].indirect(list2[:]), func=ACT.Copy)
+                nc.scalar.activation(out=pick2[:, t, :], in_=xf_sb[t].indirect(list2[:]), func=ACT.Copy)
         for t in range(0, PACK, 2):
             nc.vector.tensor_tensor(
                 out=larger[:, t : t + 2, :], in0=pick1[:, t : t + 2, :], in1=pick2[:, t : t + 2, :], op=ALU.max
@@ -139,7 +139,6 @@ def tile_list_two_largerpicks_gated_stepgap_rowabove_kernel(
             )
 
         w2s_dealt = deal_scales("w2s_dealt", w2s_raw, "pick2")
-        w2_dealt = deal_words("w2_dealt", w2_raw)
         nc.scalar.activation(out=gate[:, 1:PACK, :].rearrange("p t j -> p (t j)"), in_=so_rest[:], func=ACT.Sigmoid)
 
         def product(bank, words, scales, codes, code_scales):
@@ -166,12 +165,13 @@ def tile_list_two_largerpicks_gated_stepgap_rowabove_kernel(
             )
 
         for t in range(last):
-            nc.scalar.activation(out=entry[:, t, :], in_=xo_sb[t][:].indirect(list3[:]), func=ACT.Copy)
+            nc.scalar.activation(out=entry[:, t, :], in_=xo_sb[t].indirect(list3[:]), func=ACT.Copy)
             gate_entries(entry[:, t, :], t, slice(0, J))
-        nc.scalar.activation(out=entry_end[0][:], in_=xo_sb[last][:].indirect(list3[:, 0:8]), func=ACT.Copy)
-        nc.vector.tensor_copy(out=entry_end[1][:], in_=xo_sb[last][:].indirect(list3[:, 8:16]))
+        nc.scalar.activation(out=entry_end[0][:], in_=xo_sb[last].indirect(list3[:, 0:8]), func=ACT.Copy)
+        nc.vector.tensor_copy(out=entry_end[1][:], in_=xo_sb[last].indirect(list3[:, 8:16]))
         for h in range(2):
             gate_entries(entry_end[h][:], last, halves[h])
+        w2_dealt = deal_words("w2_dealt", w2_raw, "entry_end0")
         u2_bf = [new("u2_bf%d" % h, [P, HALF * PACK], BF16) for h in range(2)]
         for h in range(2):
             nc.vector.tensor_copy(
@@ -185,7 +185,7 @@ def tile_list_two_largerpicks_gated_stepgap_rowabove_kernel(
             nc.vector.quantize_mx(out=codes[:].bitcast(E5M2), scales=scales[:], in_=u2_bf[h][:])
             product(q_ps[h], w2_dealt, w2s_dealt, codes[:].bitcast(E5M2), scales[:])
 
-        w_dealt = deal_words("w_dealt", w_raw, "entry_end0")
+        w_dealt = deal_words("w_dealt", w_raw, "u_bf1")
         ws_dealt = deal_scales("ws_dealt", ws_raw, "u2_bf1")
         a_ps = [ps.tile([P, PACK, HALF], F32, name="a_ps%d" % h) for h in range(2)]
         for h in range(2):
@@ -195,15 +195,17 @@ def tile_list_two_largerpicks_gated_stepgap_rowabove_kernel(
         W = HALF * PACK
         step = [new("step%d" % h, [P, W], F32) for h in range(2)]
         hid_bf = [new("hid_bf%d" % h, [P, W], BF16) for h in range(2)]
-        for h in range(2):
+        pieces = [(0, 0, HALF // 2), (0, HALF // 2, HALF), (1, 0, HALF)]
+        for h, j0, j1 in pieces:
             nc.scalar.copy(
-                out=q_sb[:, PACK + W * h : PACK + W * (h + 1)].rearrange("p (j t) -> p j t", t=PACK),
-                in_=q_ps[h][:].rearrange("p t j -> p j t"),
+                out=q_sb[:, PACK * (1 + HALF * h + j0) : PACK * (1 + HALF * h + j1)].rearrange("p (j t) -> p j t", t=PACK),
+                in_=q_ps[h][:, :, j0:j1].rearrange("p t j -> p j t"),
             )
-        for h in range(2):
+        for h, j0, j1 in pieces:
             nc.vector.scalar_tensor_tensor(
-                out=step[h][:], in0=q_sb[:, W * h : W * (h + 1)], scalar=-0.6,
-                in1=q_sb[:, PACK + W * h : PACK + W * (h + 1)], op0=ALU.mult, op1=ALU.add,
+                out=step[h][:, PACK * j0 : PACK * j1],
+                in0=q_sb[:, PACK * (HALF * h + j0) : PACK * (HALF * h + j1)], scalar=-0.6,
+                in1=q_sb[:, PACK * (1 + HALF * h + j0) : PACK * (1 + HALF * h + j1)], op0=ALU.mult, op1=ALU.add,
             )
         for h in range(2):
             nc.vector.tensor_tensor(

from contextlib import ExitStack

import concourse.mybir as mybir

K, T, J, R, F, Z, N = 512, 512, 256, 512, 512, 1024, 256
FLOPS = 2 * (K * R * J + F * R * J + R * J * N)

F32 = mybir.dt.float32
BF16 = mybir.dt.bfloat16
I32 = mybir.dt.int32
U32 = mybir.dt.uint32
U16 = mybir.dt.uint16
U8 = mybir.dt.uint8
E4M3 = mybir.dt.float8_e4m3fn_x4
E5M2 = mybir.dt.float8_e5m2_x4
E2M1 = mybir.dt.float4_e2m1fn_x4
ALU = mybir.AluOpType
ACT = mybir.ActivationFunctionType

P = 128
PACK = 4
HALF = 128


def tile_list_two_largerpicks_gated_stepgap_rowabove_kernel(
    tc, xf, fk, w_words, w_scales, xo, fl, so, w2_words, w2_scales, wb_words, wb_scales, rs, offs, offs2, offs3, out
):
    nc = tc.nc
    with ExitStack() as ctx:
        sb = ctx.enter_context(tc.tile_pool(name="sb", bufs=1))
        ps = ctx.enter_context(tc.psum_pool(name="ps", bufs=1))

        def new(name, shape, dtype, tag=None):
            return sb.tile(shape, dtype, name=name, tag=tag or name, align_bytes=64)

        list1 = new("list1", [P, J // 16], U16)
        list2 = new("list2", [P, J // 16], U16)
        list3 = new("list3", [P, J // 16], U16)
        so_first = new("so_first", [P, J], F32)
        so_rest = new("so_rest", [P, (PACK - 1) * J], F32)
        xf_pair = [new("xf_pair%d" % g, [P, 2 * T], F32) for g in range(2)]
        xf_sb = [xf_pair[t // 2][:, T * (t % 2) : T * (t % 2 + 1)] for t in range(PACK)]
        xo_pair = new("xo_pair", [P, 2 * Z], F32)
        xo_single = [new("xo_single%d" % t, [P, Z], F32) for t in range(2)]
        xo_sb = [xo_pair[:, 0:Z], xo_pair[:, Z : 2 * Z], xo_single[0][:], xo_single[1][:]]
        fk_sb = new("fk_sb", [P, PACK], F32)
        fl_sb = new("fl_sb", [P, PACK], F32)
        w_raw = new("w_raw", [P, 2 * R], U8)
        w2_raw = new("w2_raw", [P, 2 * R], U8)
        wb_sb = new("wb_sb", [P, 2 * N], U8)
        ws_raw = new("ws_raw", [P, R], U8)
        w2s_raw = new("w2s_raw", [P, R], U8)
        wbs_sb = new("wbs_sb", [P, N], U8)
        rs_sb = new("rs_sb", [P, 2, N], F32)
        q_sb = new("q_sb", [P, PACK * (J + 1)], F32)

        def load_scales(queue, plane, scales, quad):
            queue.dma_start(
                out=plane[32 * quad : 32 * quad + 4, :].bitcast(I32),
                in_=scales[0, 4 * quad : 4 * quad + 4, :].bitcast(I32),
            )

        for plane in (w2s_raw, ws_raw, wbs_sb):
            nc.vector.memset(plane[:].bitcast(U32), 0)
        nc.vector.memset(q_sb[:, 0:PACK], 0.0)

        xf_rows = xf.rearrange("(p t) c -> p (t c)", t=PACK)
        xo_rows = xo.rearrange("(p t) c -> p (t c)", t=PACK)
        so_rows = so.rearrange("(p t) j -> p (t j)", t=PACK)
        for quad in range(4):
            load_scales(nc.gpsimd, w2s_raw, w2_scales, quad)
        for quad in range(4):
            load_scales(nc.gpsimd, ws_raw, w_scales, quad)
        nc.sync.dma_start(out=so_first[:], in_=so_rows[:, 0:J])
        nc.sync.dma_start(out=list1[:], in_=offs)
        nc.sync.dma_start(out=list2[:], in_=offs2)
        for g in range(2):
            nc.sync.dma_start(out=xf_pair[g][:], in_=xf_rows[:, 2 * T * g : 2 * T * (g + 1)])
        nc.sync.dma_start(out=fk_sb[:], in_=fk.rearrange("(p t) o -> p (t o)", t=PACK))
        nc.sync.dma_start(out=so_rest[:], in_=so_rows[:, J : PACK * J])
        nc.sync.dma_start(out=list3[:], in_=offs3)
        nc.sync.dma_start(out=xo_pair[:], in_=xo_rows[:, 0 : 2 * Z])
        nc.sync.dma_start(out=fl_sb[:], in_=fl.rearrange("(p t) o -> p (t o)", t=PACK))
        for t in range(2):
            nc.sync.dma_start(out=xo_single[t][:], in_=xo_rows[:, Z * (2 + t) : Z * (3 + t)])
        nc.sync.dma_start(out=w2_raw[:].bitcast(I32), in_=w2_words[0].bitcast(I32))
        nc.sync.dma_start(out=w_raw[:].bitcast(I32), in_=w_words[0].bitcast(I32))
        nc.sync.dma_start(out=wb_sb[:].bitcast(I32), in_=wb_words[0].bitcast(I32))
        for quad in range(4):
            load_scales(nc.sync, wbs_sb, wb_scales, quad)
        nc.sync.dma_start(out=rs_sb[:], in_=rs.rearrange("(h p) n -> p h n", p=P))

        def deal_words(name, raw_words, tag=None):
            words = new(name, [P, 2 * R], U8, tag)
            nc.scalar.copy(
                out=words[:].bitcast(U16).rearrange("p (t m) -> p t m", t=PACK),
                in_=raw_words[:].bitcast(U16).rearrange("p (m t) -> p t m", t=PACK),
            )
            return words

        def deal_scales(name, raw_scales, tag):
            scales = new(name, [P, R], U8, tag)
            nc.vector.tensor_copy(
                out=scales[:].rearrange("p (t m) -> p t m", t=PACK),
                in_=raw_scales[:].rearrange("p (m t) -> p t m", t=PACK),
            )
            return scales

        gate = new("gate", [P, PACK, J], F32)
        nc.scalar.activation(out=gate[:, 0, :], in_=so_first[:], func=ACT.Sigmoid)

        pick1 = new("pick1", [P, PACK, J], F32)
        pick2 = new("pick2", [P, PACK, J], F32)
        larger = new("larger", [P, PACK, J], F32)
        for t in range(PACK):
            nc.scalar.activation(out=pick1[:, t, :], in_=xf_sb[t].indirect(list1[:]), func=ACT.Copy)
            if t < PACK - 1:
                nc.vector.tensor_copy(out=pick2[:, t, :], in_=xf_sb[t].indirect(list2[:]))
            else:
                nc.scalar.activation(out=pick2[:, t, :], in_=xf_sb[t].indirect(list2[:]), func=ACT.Copy)
        for t in range(0, PACK, 2):
            nc.vector.tensor_tensor(
                out=larger[:, t : t + 2, :], in0=pick1[:, t : t + 2, :], in1=pick2[:, t : t + 2, :], op=ALU.max
            )
        halves = [slice(HALF * h, HALF * (h + 1)) for h in range(2)]
        u_bf = [new("u_bf%d" % h, [P, HALF * PACK], BF16) for h in range(2)]
        u_codes = new("u_codes", [P, J], U32)
        u_scales = new("u_scales", [P, J], U8)
        for h in range(2):
            nc.vector.tensor_tensor(
                out=u_bf[h][:].rearrange("p (c i t) -> p c t i", i=4, t=PACK),
                in0=larger[:, :, halves[h]].rearrange("p t (c i) -> p c t i", i=4),
                in1=fk_sb[:].unsqueeze(1).unsqueeze(3).to_broadcast([P, HALF // 4, PACK, 4]),
                op=ALU.mult,
            )
        for h in range(2):
            nc.vector.quantize_mx(
                out=u_codes[:, halves[h]].bitcast(E4M3), scales=u_scales[:, halves[h]], in_=u_bf[h][:]
            )

        w2s_dealt = deal_scales("w2s_dealt", w2s_raw, "pick2")
        nc.scalar.activation(out=gate[:, 1:PACK, :].rearrange("p t j -> p (t j)"), in_=so_rest[:], func=ACT.Sigmoid)

        def product(bank, words, scales, codes, code_scales):
            for t in range(PACK):
                nc.tensor.matmul_mx(
                    out=bank[:, t, :],
                    lhsT=words[:, 2 * P * t : 2 * P * (t + 1)].bitcast(E2M1),
                    lhsT_scale=scales[:, P * t : P * (t + 1)],
                    rhs=codes,
                    rhs_scale=code_scales,
                    start=True,
                    stop=True,
                )

        last = PACK - 1
        entry = new("entry", [P, last, J], F32)
        entry_end = [new("entry_end0", [P, HALF], F32), new("entry_end1", [P, HALF], F32, "u_bf1")]
        gated = new("gated", [P, PACK, J], F32, "u_bf0")

        def gate_entries(picked, t, cols):
            nc.vector.scalar_tensor_tensor(
                out=gated[:, t, cols], in0=picked, scalar=fl_sb[:, t : t + 1], in1=gate[:, t, cols],
                op0=ALU.mult, op1=ALU.mult,
            )

        for t in range(last):
            nc.scalar.activation(out=entry[:, t, :], in_=xo_sb[t].indirect(list3[:]), func=ACT.Copy)
            gate_entries(entry[:, t, :], t, slice(0, J))
        nc.scalar.activation(out=entry_end[0][:], in_=xo_sb[last].indirect(list3[:, 0:8]), func=ACT.Copy)
        nc.vector.tensor_copy(out=entry_end[1][:], in_=xo_sb[last].indirect(list3[:, 8:16]))
        for h in range(2):
            gate_entries(entry_end[h][:], last, halves[h])
        w2_dealt = deal_words("w2_dealt", w2_raw, "entry_end0")
        u2_bf = [new("u2_bf%d" % h, [P, HALF * PACK], BF16) for h in range(2)]
        for h in range(2):
            nc.vector.tensor_copy(
                out=u2_bf[h][:].rearrange("p (c i t) -> p c t i", i=4, t=PACK),
                in_=gated[:, :, halves[h]].rearrange("p t (c i) -> p c t i", i=4),
            )
        q_ps = [ps.tile([P, PACK, HALF], F32, name="q_ps%d" % h) for h in range(2)]
        for h in range(2):
            codes = new("u2_codes%d" % h, [P, HALF], U32)
            scales = new("u2_scales%d" % h, [P, HALF], U8)
            nc.vector.quantize_mx(out=codes[:].bitcast(E5M2), scales=scales[:], in_=u2_bf[h][:])
            product(q_ps[h], w2_dealt, w2s_dealt, codes[:].bitcast(E5M2), scales[:])

        w_dealt = deal_words("w_dealt", w_raw, "u_bf1")
        ws_dealt = deal_scales("ws_dealt", ws_raw, "u2_bf1")
        a_ps = [ps.tile([P, PACK, HALF], F32, name="a_ps%d" % h) for h in range(2)]
        for h in range(2):
            cols = slice(HALF * h, HALF * (h + 1))
            product(a_ps[h], w_dealt, ws_dealt, u_codes[:, cols].bitcast(E4M3), u_scales[:, cols])

        W = HALF * PACK
        step = [new("step%d" % h, [P, W], F32) for h in range(2)]
        hid_bf = [new("hid_bf%d" % h, [P, W], BF16) for h in range(2)]
        pieces = [(0, 0, HALF // 2), (0, HALF // 2, HALF), (1, 0, HALF)]
        for h, j0, j1 in pieces:
            nc.scalar.copy(
                out=q_sb[:, PACK * (1 + HALF * h + j0) : PACK * (1 + HALF * h + j1)].rearrange("p (j t) -> p j t", t=PACK),
                in_=q_ps[h][:, :, j0:j1].rearrange("p t j -> p j t"),
            )
        for h, j0, j1 in pieces:
            nc.vector.scalar_tensor_tensor(
                out=step[h][:, PACK * j0 : PACK * j1],
                in0=q_sb[:, PACK * (HALF * h + j0) : PACK * (HALF * h + j1)], scalar=-0.6,
                in1=q_sb[:, PACK * (1 + HALF * h + j0) : PACK * (1 + HALF * h + j1)], op0=ALU.mult, op1=ALU.add,
            )
        for h in range(2):
            nc.vector.tensor_tensor(
                out=hid_bf[h][:].rearrange("p (j t) -> p j t", t=PACK),
                in0=a_ps[h][:].rearrange("p t j -> p j t"),
                in1=step[h][:].rearrange("p (j t) -> p j t", t=PACK),
                op=ALU.max,
            )
        p_ps = [ps.tile([P, N], F32, name="p_ps%d" % h) for h in range(2)]
        for h in range(2):
            codes = new("hid_codes%d" % h, [P, HALF], U32)
            scales = new("hid_scales%d" % h, [P, HALF], U8)
            nc.vector.quantize_mx(out=codes[:].bitcast(E5M2), scales=scales[:], in_=hid_bf[h][:])
            nc.tensor.matmul_mx(
                out=p_ps[h][:], lhsT=codes[:].bitcast(E5M2), lhsT_scale=scales[:],
                rhs=wb_sb[:].bitcast(E2M1), rhs_scale=wbs_sb[:], start=True, stop=True,
            )
        mean = [new("mean%d" % h, [P, 1], F32) for h in range(2)]
        result = [new("result%d" % h, [P, N], F32) for h in range(2)]
        for h in range(2):
            magnitude = new("magnitude%d" % h, [P, N], F32)
            nc.scalar.activation(out=magnitude[:], in_=p_ps[h][:], func=ACT.Abs, scale=1.0 / N, accum_out=mean[h][:])
        above = new("above", [P, N], F32)
        nc.vector.tensor_scalar(
            out=above[:], in0=p_ps[0][:], scalar1=mean[0][:], scalar2=0.0, op0=ALU.subtract, op1=ALU.max
        )
        nc.vector.scalar_tensor_tensor(
            out=result[0][:], in0=rs_sb[:, 0, :], scalar=-0.3, in1=above[:], op0=ALU.mult, op1=ALU.add
        )
        nc.sync.dma_start(out=out[halves[0], :], in_=result[0][:])
        taken = new("taken", [P, N], F32)
        nc.scalar.activation(out=taken[:], in_=rs_sb[:, 1, :], func=ACT.Identity, scale=0.3, bias=mean[1][:])
        nc.vector.scalar_tensor_tensor(
            out=result[1][:], in0=p_ps[1][:], scalar=mean[1][:], in1=taken[:], op0=ALU.max, op1=ALU.subtract
        )
        nc.sync.dma_start(out=out[halves[1], :], in_=result[1][:])
